import numpy as np
import ml_dtypes


def mxq(x, axis, fmt="e4m3"):
    dtype, down = {"e4m3": (ml_dtypes.float8_e4m3fn, 7), "e5m2": (ml_dtypes.float8_e5m2, 14)}[fmt]
    v = np.moveaxis(np.asarray(x, np.float32).astype(ml_dtypes.bfloat16).astype(np.float64), axis, -1)
    blocks = v.reshape(v.shape[:-1] + (-1, 32))
    amax = np.abs(blocks).max(-1, keepdims=True)
    byte = np.maximum(np.where(amax > 0, np.frexp(amax)[1] - 1 + 127, 0) - down, 1)
    scale = np.exp2(byte - 127.0)
    codes = (blocks / scale).astype(np.float32).astype(dtype).astype(np.float64)
    return np.moveaxis((codes * scale).reshape(v.shape), -1, axis)


WIDE = False


def mx_kscale(k):
    if not WIDE:
        return np.ones(k)
    levels = np.array([10, -10, 5, -5, 0])
    if k % 512:
        return np.exp2(np.random.permutation(np.resize(levels, k // 32))).repeat(32)
    a = np.empty((k // 512, 16))
    for p in range(k // 512):
        a[p, :8] = np.random.permutation(np.resize(levels, 8))
        for g in range(8):
            far = levels[np.abs(levels - a[p, g]) >= 10]
            a[p, g + 8] = far[np.random.randint(len(far))]
    return np.exp2(a.ravel()).repeat(32)


def f64(x):
    return np.asarray(x).astype(np.float64)


def striped(idx):
    return np.tile(idx.reshape(-1, 16).T, (8, 1)).astype(np.uint16)


def unstriped(offs):
    return offs[:16].T.reshape(-1).astype(np.int64)


E2M1 = np.array([0.0, 0.5, 1.0, 1.5, 2.0, 3.0, 4.0, 6.0, -0.0, -0.5, -1.0, -1.5, -2.0, -3.0, -4.0, -6.0])


def pack_weight(w, fmt):
    k, n = w.shape
    w = f64(np.asarray(w, np.float32).astype(ml_dtypes.bfloat16)).reshape(k // 32, 32, n)
    amax = np.abs(w).max(1)
    if fmt == "e4m3":
        byte = np.frexp(amax)[1] - 1 + 127 - 7
    else:
        mant, ex = np.frexp(amax / 6.0)
        byte = np.where(mant > 0.5, ex, ex - 1) + 127
    byte = np.clip(np.where(amax > 0, byte, 1), 1, 254)
    scaled = (w * np.exp2(127.0 - byte)[:, None, :]).reshape(k, n).astype(np.float32)
    by_word = np.ascontiguousarray(scaled.reshape(k // 512, 128, 4, n).transpose(0, 1, 3, 2))
    if fmt == "e4m3":
        words = by_word.astype(ml_dtypes.float8_e4m3fn).view(np.uint8)
    else:
        c = by_word.astype(ml_dtypes.float4_e2m1fn).view(np.uint8) & 0xF
        words = (c[..., 0::2] | (c[..., 1::2] << 4)).reshape(k // 512, 128, 2 * n)
    return np.ascontiguousarray(words), np.ascontiguousarray(byte.astype(np.uint8).reshape(k // 512, 16, n))


def unpack_weight(words, scales, fmt):
    g, _, n = scales.shape
    words = np.ascontiguousarray(words).reshape(g, 128, n, -1)
    if fmt == "e4m3":
        vals = words.view(ml_dtypes.float8_e4m3fn).astype(np.float64)
    else:
        nib = np.empty((g, 128, n, 4), np.uint8)
        nib[..., 0::2] = words & 0xF
        nib[..., 1::2] = words >> 4
        vals = E2M1[nib]
    vals = vals * np.repeat(np.exp2(scales.astype(np.float64) - 127.0), 8, axis=1)[..., None]
    return vals.transpose(0, 1, 3, 2).reshape(g * 512, n)


K, T, E, C, N = 1024, 768, 12, 128, 128
R = 2


def by_expert(wq, xq):
    return np.concatenate([wq[e].T @ xq[:, e * C:(e + 1) * C] for e in range(E)], axis=1)


def setup_inputs():
    n = np.random.standard_normal
    s = mx_kscale(K)[:, None]
    slot_token = np.concatenate([r * (T // R) + np.random.permutation(T // R)[:C // R] for e in range(E) for r in range(R)])
    w = [pack_weight(m, "e2m1") for m in n((E, K, N)) / np.sqrt(K) / s[None]]
    return {
        "xT": (n((K, T)) * s).astype(np.float32),
        "w_words": np.stack([m[0] for m in w]),
        "w_scales": np.stack([m[1] for m in w]),
        "b": (0.3 * n((N, E))).astype(np.float32),
        "offs": striped(slot_token),
    }


def reference(xT, w_words, w_scales, b, offs):
    idx = unstriped(offs)
    w = np.stack([unpack_weight(w_words[e], w_scales[e], "e2m1") for e in range(E)])
    xq = mxq(f64(xT)[:, idx], 0, "e4m3")
    y = by_expert(w, xq)
    y = y + np.repeat(f64(b), C, axis=1)
    return y.reshape(N, E, R, C // R).transpose(0, 2, 1, 3).reshape(N, E * C)

@@ -1,0 +1,163 @@
+from contextlib import ExitStack
+
+import concourse.mybir as mybir
+
+K, T, E, C, N, R = 1024, 768, 12, 128, 128, 2
+P = 128
+PASSES = 2
+S = E * C
+U = C // R
+FLOPS = 2 * S * K * N
+
+F32 = mybir.dt.float32
+BF16 = mybir.dt.bfloat16
+I32 = mybir.dt.int32
+U32 = mybir.dt.uint32
+U16 = mybir.dt.uint16
+U8 = mybir.dt.uint8
+FP8X4 = mybir.dt.float8_e4m3fn_x4
+FP4X4 = mybir.dt.float4_e2m1fn_x4
+COPY = mybir.ActivationFunctionType.Copy
+IDENTITY = mybir.ActivationFunctionType.Identity
+
+G = 4
+GC = G * C
+
+
+def tile_moe_eps_lin_bias_kernel(tc, xT, w_words, w_scales, b, offs, out):
+    nc = tc.nc
+    with ExitStack() as ctx:
+        keep = ctx.enter_context(tc.tile_pool(name="keep", bufs=1))
+        psum = ctx.enter_context(tc.psum_pool(name="psum", bufs=8))
+
+        offsets = keep.tile([P, S // 16], U16, name="offsets")
+        plane = keep.tile([P, T], U8, name="plane", align_bytes=64)
+        w_codes = keep.tile([P, E * PASSES, 2 * N], U8, name="w_codes", align_bytes=64)
+        w_plane = keep.tile([P, E * PASSES, N], U8, name="w_plane", align_bytes=64)
+        bias = keep.tile([P, E], F32, name="bias")
+        codes = [keep.tile([P, T], U32, name=f"codes{a}", align_bytes=64) for a in range(PASSES)]
+        slot_codes = [keep.tile([P, S], U32, name=f"slot_codes{a}", align_bytes=64) for a in range(PASSES)]
+        slot_plane = keep.tile([P, S], U8, name="slot_plane", align_bytes=64)
+        slot_plane1 = keep.tile([P, S], U8, name="slot_plane1", align_bytes=64)
+        rounded = [keep.tile([P, T, 4], BF16, name=f"rounded{a}", align_bytes=64) for a in range(PASSES)]
+
+        nc.gpsimd.memset(plane[:].bitcast(I32), 0)
+        nc.gpsimd.memset(slot_plane1[:].bitcast(I32), 0)
+        nc.gpsimd.memset(w_plane[:].rearrange("p a n -> p (a n)").bitcast(I32), 0)
+
+        raw = {}
+
+        def load(a, c0, c1):
+            t = keep.tile([P, 4, c1 - c0], F32, name=f"raw{a}_{c0}")
+            nc.sync.dma_start(t[:], xT[512 * a : 512 * a + 512, c0:c1].rearrange("(p j) w -> p j w", j=4))
+            raw[a, c0] = t
+
+        def cast(engine, a, base, c0, c1):
+            src = raw[a, base][:, :, c0 - base : c1 - base].rearrange("p j w -> p w j")
+            dst = rounded[a][:, c0:c1, :]
+            if engine == "v":
+                nc.vector.tensor_copy(dst, src)
+            else:
+                nc.scalar.activation(dst, src, COPY)
+
+        def quantise(a, c0, c1):
+            nc.vector.quantize_mx(
+                out=codes[a][:, c0:c1].bitcast(FP8X4),
+                scales=plane[4 * a : P, c0:c1],
+                in_=rounded[a][:, c0:c1, :].rearrange("p w j -> p (w j)"),
+            )
+
+        load(0, 0, 512)
+        load(0, 512, 768)
+        nc.sync.dma_start(offsets[:], offs)
+        load(1, 0, 256)
+        load(1, 256, 512)
+        load(1, 512, 768)
+        for h in range(2):
+            es = slice(h * E // 2, (h + 1) * E // 2)
+            ts = slice(h * E, (h + 1) * E)
+            nc.sync.dma_start(w_codes[:, ts, :].bitcast(I32), w_words[es].rearrange("e a p b -> p (e a) b").bitcast(I32))
+        for q in range(4):
+            nc.sync.dma_start(
+                w_plane[32 * q : 32 * q + 4, :, :].bitcast(I32),
+                w_scales[:, :, 4 * q : 4 * q + 4, :].rearrange("e a r n -> r (e a) n").bitcast(I32),
+            )
+        nc.sync.dma_start(bias[:], b)
+
+        cast("v", 0, 0, 0, 320)
+        cast("s", 0, 0, 320, 512)
+        quantise(0, 0, 512)
+        cast("v", 0, 512, 512, 672)
+        cast("s", 0, 512, 672, 768)
+        quantise(0, 512, 768)
+
+        def gather_codes(a, s0, s1):
+            nc.vector.tensor_copy(slot_codes[a][:, s0:s1], codes[a][:].indirect(offsets[:, s0 // 16 : s1 // 16]))
+
+        def gather_scales(s0, s1):
+            nc.vector.tensor_copy(slot_plane[:, s0:s1], plane[:].indirect(offsets[:, s0 // 16 : s1 // 16]))
+            for q in range(4):
+                nc.sync.dma_start(
+                    slot_plane1[32 * q : 32 * q + 4, s0:s1].bitcast(I32),
+                    slot_plane[32 * q + 4 : 32 * q + 8, s0:s1].bitcast(I32),
+                )
+
+        for s0 in range(0, S, GC):
+            gather_codes(0, s0, s0 + GC)
+        for c0 in range(0, T, 256):
+            cast("s", 1, c0, c0, c0 + 256)
+        quantise(1, 0, 512)
+        quantise(1, 512, 768)
+        for s0 in range(0, S, GC):
+            gather_scales(s0, s0 + GC)
+
+        acc = {}
+        scales = [slot_plane, slot_plane1]
+
+        def multiply(e, a):
+            if a == 0:
+                acc[e] = psum.tile([P, C], F32, name="acc")
+            cols = slice(e * C, (e + 1) * C)
+            nc.tensor.matmul_mx(
+                out=acc[e][:],
+                lhsT=w_codes[:, e * PASSES + a, :].bitcast(FP4X4),
+                lhsT_scale=w_plane[:, e * PASSES + a, :],
+                rhs=slot_codes[a][:, cols].bitcast(FP8X4),
+                rhs_scale=scales[a][:, cols],
+                start=(a == 0),
+                stop=(a == PASSES - 1),
+            )
+
+        out_view = out.rearrange("n (m e u) -> n m e u", m=R, e=E)
+
+        def finish(e0, e1, on_vector):
+            y = keep.tile([P, R, e1 - e0, U], F32, name=f"y{e0}")
+            for e in range(e0, e1):
+                dst = y[:, :, e - e0, :]
+                src = acc[e][:].rearrange("p (m u) -> p m u", m=R)
+                if e in on_vector:
+                    nc.vector.tensor_scalar_add(dst, src, bias[:, e : e + 1])
+                else:
+                    nc.scalar.activation(dst, src, IDENTITY, bias=bias[:, e : e + 1])
+            nc.sync.dma_start(out_view[:, :, e0:e1, :], y[:])
+
+        for e in range(8):
+            multiply(e, 0)
+        gather_codes(1, 0, 512)
+        for e in range(4):
+            multiply(e, 1)
+        finish(0, 4, ())
+        for e in range(8, 12):
+            multiply(e, 0)
+        gather_codes(1, 512, 1024)
+        for e in range(4, 8):
+            multiply(e, 1)
+        finish(4, 8, ())
+        gather_codes(1, 1024, 1280)
+        for e in range(8, 10):
+            multiply(e, 1)
+        finish(8, 10, ())
+        gather_codes(1, 1280, 1536)
+        for e in range(10, 12):
+            multiply(e, 1)
+        finish(10, 12, (11,))

@@ -20,8 +20,7 @@ FP4X4 = mybir.dt.float4_e2m1fn_x4
 COPY = mybir.ActivationFunctionType.Copy
 IDENTITY = mybir.ActivationFunctionType.Identity
 
-G = 4
-GC = G * C
+W = 1024
 
 
 def tile_moe_eps_lin_bias_kernel(tc, xT, w_words, w_scales, b, offs, out):
@@ -31,17 +30,19 @@ def tile_moe_eps_lin_bias_kernel(tc, xT, w_words, w_scales, b, offs, out):
         psum = ctx.enter_context(tc.psum_pool(name="psum", bufs=8))
 
         offsets = keep.tile([P, S // 16], U16, name="offsets")
-        plane = keep.tile([P, T], U8, name="plane", align_bytes=64)
+        plane = keep.tile([P, W], U8, name="plane", align_bytes=64)
         w_codes = keep.tile([P, E * PASSES, 2 * N], U8, name="w_codes", align_bytes=64)
         w_plane = keep.tile([P, E * PASSES, N], U8, name="w_plane", align_bytes=64)
         bias = keep.tile([P, E], F32, name="bias")
-        codes = [keep.tile([P, T], U32, name=f"codes{a}", align_bytes=64) for a in range(PASSES)]
+        codes = [keep.tile([P, w], U32, name=f"codes{a}", align_bytes=64) for a, w in enumerate((2 * W, W))]
         slot_codes = [keep.tile([P, S], U32, name=f"slot_codes{a}", align_bytes=64) for a in range(PASSES)]
         slot_plane = keep.tile([P, S], U8, name="slot_plane", align_bytes=64)
         slot_plane1 = keep.tile([P, S], U8, name="slot_plane1", align_bytes=64)
         rounded = [keep.tile([P, T, 4], BF16, name=f"rounded{a}", align_bytes=64) for a in range(PASSES)]
 
         nc.gpsimd.memset(plane[:].bitcast(I32), 0)
+        for a in range(PASSES):
+            nc.gpsimd.memset(codes[a][:, T:].bitcast(I32), 0)
         nc.gpsimd.memset(slot_plane1[:].bitcast(I32), 0)
         nc.gpsimd.memset(w_plane[:].rearrange("p a n -> p (a n)").bitcast(I32), 0)
 
@@ -53,8 +54,8 @@ def tile_moe_eps_lin_bias_kernel(tc, xT, w_words, w_scales, b, offs, out):
             raw[a, c0] = t
 
         def cast(engine, a, base, c0, c1):
-            src = raw[a, base][:, :, c0 - base : c1 - base].rearrange("p j w -> p w j")
-            dst = rounded[a][:, c0:c1, :]
+            src = raw[a, base][:, :, c0 - base : c1 - base].rearrange("p j (c i) -> p c j i", i=4)
+            dst = rounded[a][:, c0:c1, :].rearrange("p (c i) j -> p c j i", i=4)
             if engine == "v":
                 nc.vector.tensor_copy(dst, src)
             else:
@@ -84,11 +85,12 @@ def tile_moe_eps_lin_bias_kernel(tc, xT, w_words, w_scales, b, offs, out):
             )
         nc.sync.dma_start(bias[:], b)
 
-        cast("v", 0, 0, 0, 320)
-        cast("s", 0, 0, 320, 512)
-        quantise(0, 0, 512)
+        cast("v", 0, 0, 0, 256)
+        cast("s", 0, 0, 256, 512)
+        quantise(0, 0, 256)
         cast("v", 0, 512, 512, 672)
         cast("s", 0, 512, 672, 768)
+        quantise(0, 256, 512)
         quantise(0, 512, 768)
 
         def gather_codes(a, s0, s1):
@@ -102,14 +104,14 @@ def tile_moe_eps_lin_bias_kernel(tc, xT, w_words, w_scales, b, offs, out):
                     slot_plane[32 * q + 4 : 32 * q + 8, s0:s1].bitcast(I32),
                 )
 
-        for s0 in range(0, S, GC):
-            gather_codes(0, s0, s0 + GC)
-        for c0 in range(0, T, 256):
-            cast("s", 1, c0, c0, c0 + 256)
+        gather_codes(0, 0, S)
+        cast("s", 1, 0, 0, 256)
+        cast("s", 1, 256, 256, 512)
         quantise(1, 0, 512)
+        cast("s", 1, 512, 512, 768)
         quantise(1, 512, 768)
-        for s0 in range(0, S, GC):
-            gather_scales(s0, s0 + GC)
+        for s0 in range(0, S, 512):
+            gather_scales(s0, s0 + 512)
 
         acc = {}
         scales = [slot_plane, slot_plane1]
@@ -143,21 +145,12 @@ def tile_moe_eps_lin_bias_kernel(tc, xT, w_words, w_scales, b, offs, out):
 
         for e in range(8):
             multiply(e, 0)
-        gather_codes(1, 0, 512)
-        for e in range(4):
-            multiply(e, 1)
-        finish(0, 4, ())
-        for e in range(8, 12):
-            multiply(e, 0)
-        gather_codes(1, 512, 1024)
-        for e in range(4, 8):
-            multiply(e, 1)
-        finish(4, 8, ())
-        gather_codes(1, 1024, 1280)
-        for e in range(8, 10):
-            multiply(e, 1)
-        finish(8, 10, ())
-        gather_codes(1, 1280, 1536)
-        for e in range(10, 12):
-            multiply(e, 1)
-        finish(10, 12, (11,))
+        opened = 8
+        for e0, e1, ahead in ((0, 4, 4), (4, 8, 0), (8, 10, 0), (10, 12, 0)):
+            gather_codes(1, e0 * C, e1 * C)
+            for e in range(e0, e1):
+                multiply(e, 1)
+            finish(e0, e1, (11,))
+            for e in range(opened, opened + ahead):
+                multiply(e, 0)
+            opened += ahead

from contextlib import ExitStack

import concourse.mybir as mybir

K, T, E, C, N, R = 1024, 768, 12, 128, 128, 2
P = 128
PASSES = 2
S = E * C
U = C // R
FLOPS = 2 * S * K * N

F32 = mybir.dt.float32
BF16 = mybir.dt.bfloat16
I32 = mybir.dt.int32
U32 = mybir.dt.uint32
U16 = mybir.dt.uint16
U8 = mybir.dt.uint8
FP8X4 = mybir.dt.float8_e4m3fn_x4
FP4X4 = mybir.dt.float4_e2m1fn_x4
COPY = mybir.ActivationFunctionType.Copy
IDENTITY = mybir.ActivationFunctionType.Identity

W = 1024


def tile_moe_eps_lin_bias_kernel(tc, xT, w_words, w_scales, b, offs, out):
    nc = tc.nc
    with ExitStack() as ctx:
        keep = ctx.enter_context(tc.tile_pool(name="keep", bufs=1))
        psum = ctx.enter_context(tc.psum_pool(name="psum", bufs=8))

        offsets = keep.tile([P, S // 16], U16, name="offsets")
        plane = keep.tile([P, W], U8, name="plane", align_bytes=64)
        w_codes = keep.tile([P, E * PASSES, 2 * N], U8, name="w_codes", align_bytes=64)
        w_plane = keep.tile([P, E * PASSES, N], U8, name="w_plane", align_bytes=64)
        bias = keep.tile([P, E], F32, name="bias")
        codes = [keep.tile([P, w], U32, name=f"codes{a}", align_bytes=64) for a, w in enumerate((2 * W, W))]
        slot_codes = [keep.tile([P, S], U32, name=f"slot_codes{a}", align_bytes=64) for a in range(PASSES)]
        slot_plane = keep.tile([P, S], U8, name="slot_plane", align_bytes=64)
        slot_plane1 = keep.tile([P, S], U8, name="slot_plane1", align_bytes=64)
        rounded = [keep.tile([P, T, 4], BF16, name=f"rounded{a}", align_bytes=64) for a in range(PASSES)]

        nc.gpsimd.memset(plane[:].bitcast(I32), 0)
        for a in range(PASSES):
            nc.gpsimd.memset(codes[a][:, T:].bitcast(I32), 0)
        nc.gpsimd.memset(slot_plane1[:].bitcast(I32), 0)
        nc.gpsimd.memset(w_plane[:].rearrange("p a n -> p (a n)").bitcast(I32), 0)

        raw = {}

        def load(a, c0, c1):
            t = keep.tile([P, 4, c1 - c0], F32, name=f"raw{a}_{c0}")
            nc.sync.dma_start(t[:], xT[512 * a : 512 * a + 512, c0:c1].rearrange("(p j) w -> p j w", j=4))
            raw[a, c0] = t

        def cast(engine, a, base, c0, c1):
            src = raw[a, base][:, :, c0 - base : c1 - base].rearrange("p j (c i) -> p c j i", i=4)
            dst = rounded[a][:, c0:c1, :].rearrange("p (c i) j -> p c j i", i=4)
            if engine == "v":
                nc.vector.tensor_copy(dst, src)
            else:
                nc.scalar.activation(dst, src, COPY)

        def quantise(a, c0, c1):
            nc.vector.quantize_mx(
                out=codes[a][:, c0:c1].bitcast(FP8X4),
                scales=plane[4 * a : P, c0:c1],
                in_=rounded[a][:, c0:c1, :].rearrange("p w j -> p (w j)"),
            )

        load(0, 0, 512)
        load(0, 512, 768)
        nc.sync.dma_start(offsets[:], offs)
        load(1, 0, 256)
        load(1, 256, 512)
        load(1, 512, 768)
        for h in range(2):
            es = slice(h * E // 2, (h + 1) * E // 2)
            ts = slice(h * E, (h + 1) * E)
            nc.sync.dma_start(w_codes[:, ts, :].bitcast(I32), w_words[es].rearrange("e a p b -> p (e a) b").bitcast(I32))
        for q in range(4):
            nc.sync.dma_start(
                w_plane[32 * q : 32 * q + 4, :, :].bitcast(I32),
                w_scales[:, :, 4 * q : 4 * q + 4, :].rearrange("e a r n -> r (e a) n").bitcast(I32),
            )
        nc.sync.dma_start(bias[:], b)

        cast("v", 0, 0, 0, 256)
        cast("s", 0, 0, 256, 512)
        quantise(0, 0, 256)
        cast("v", 0, 512, 512, 672)
        cast("s", 0, 512, 672, 768)
        quantise(0, 256, 512)
        quantise(0, 512, 768)

        def gather_codes(a, s0, s1):
            nc.vector.tensor_copy(slot_codes[a][:, s0:s1], codes[a][:].indirect(offsets[:, s0 // 16 : s1 // 16]))

        def gather_scales(s0, s1):
            nc.vector.tensor_copy(slot_plane[:, s0:s1], plane[:].indirect(offsets[:, s0 // 16 : s1 // 16]))
            for q in range(4):
                nc.sync.dma_start(
                    slot_plane1[32 * q : 32 * q + 4, s0:s1].bitcast(I32),
                    slot_plane[32 * q + 4 : 32 * q + 8, s0:s1].bitcast(I32),
                )

        gather_codes(0, 0, S)
        cast("s", 1, 0, 0, 256)
        cast("s", 1, 256, 256, 512)
        quantise(1, 0, 512)
        cast("s", 1, 512, 512, 768)
        quantise(1, 512, 768)
        for s0 in range(0, S, 512):
            gather_scales(s0, s0 + 512)

        acc = {}
        scales = [slot_plane, slot_plane1]

        def multiply(e, a):
            if a == 0:
                acc[e] = psum.tile([P, C], F32, name="acc")
            cols = slice(e * C, (e + 1) * C)
            nc.tensor.matmul_mx(
                out=acc[e][:],
                lhsT=w_codes[:, e * PASSES + a, :].bitcast(FP4X4),
                lhsT_scale=w_plane[:, e * PASSES + a, :],
                rhs=slot_codes[a][:, cols].bitcast(FP8X4),
                rhs_scale=scales[a][:, cols],
                start=(a == 0),
                stop=(a == PASSES - 1),
            )

        out_view = out.rearrange("n (m e u) -> n m e u", m=R, e=E)

        def finish(e0, e1, on_vector):
            y = keep.tile([P, R, e1 - e0, U], F32, name=f"y{e0}")
            for e in range(e0, e1):
                dst = y[:, :, e - e0, :]
                src = acc[e][:].rearrange("p (m u) -> p m u", m=R)
                if e in on_vector:
                    nc.vector.tensor_scalar_add(dst, src, bias[:, e : e + 1])
                else:
                    nc.scalar.activation(dst, src, IDENTITY, bias=bias[:, e : e + 1])
            nc.sync.dma_start(out_view[:, :, e0:e1, :], y[:])

        for e in range(8):
            multiply(e, 0)
        opened = 8
        for e0, e1, ahead in ((0, 4, 4), (4, 8, 0), (8, 10, 0), (10, 12, 0)):
            gather_codes(1, e0 * C, e1 * C)
            for e in range(e0, e1):
                multiply(e, 1)
            finish(e0, e1, (11,))
            for e in range(opened, opened + ahead):
                multiply(e, 0)
            opened += ahead
